import numpy as np
import ml_dtypes


def mxq(x, axis, fmt="e4m3"):
    dtype, down = {"e4m3": (ml_dtypes.float8_e4m3fn, 7), "e5m2": (ml_dtypes.float8_e5m2, 14)}[fmt]
    v = np.moveaxis(np.asarray(x, np.float32).astype(ml_dtypes.bfloat16).astype(np.float64), axis, -1)
    blocks = v.reshape(v.shape[:-1] + (-1, 32))
    amax = np.abs(blocks).max(-1, keepdims=True)
    byte = np.maximum(np.where(amax > 0, np.frexp(amax)[1] - 1 + 127, 0) - down, 1)
    scale = np.exp2(byte - 127.0)
    codes = (blocks / scale).astype(np.float32).astype(dtype).astype(np.float64)
    return np.moveaxis((codes * scale).reshape(v.shape), -1, axis)


WIDE = False


def mx_kscale(k):
    if not WIDE:
        return np.ones(k)
    levels = np.array([10, -10, 5, -5, 0])
    if k % 512:
        return np.exp2(np.random.permutation(np.resize(levels, k // 32))).repeat(32)
    a = np.empty((k // 512, 16))
    for p in range(k // 512):
        a[p, :8] = np.random.permutation(np.resize(levels, 8))
        for g in range(8):
            far = levels[np.abs(levels - a[p, g]) >= 10]
            a[p, g + 8] = far[np.random.randint(len(far))]
    return np.exp2(a.ravel()).repeat(32)


def f64(x):
    return np.asarray(x).astype(np.float64)


def striped(idx):
    return np.tile(idx.reshape(-1, 16).T, (8, 1)).astype(np.uint16)


def unstriped(offs):
    return offs[:16].T.reshape(-1).astype(np.int64)


def relu2(v):
    return np.maximum(v, 0.0) ** 2


K, T, E, C, N = 512, 1536, 12, 256, 128


def by_expert(wq, xq):
    return np.concatenate([wq[e].T @ xq[:, e * C:(e + 1) * C] for e in range(E)], axis=1)


def setup_inputs():
    n = np.random.standard_normal
    s = mx_kscale(K)[:, None]
    first = np.random.permutation(np.repeat(np.arange(E), T // E))
    second = (first + 1 + np.random.permutation(np.repeat(np.arange(E - 1), -(-T // (E - 1)))[:T])) % E
    while np.bincount(second, minlength=E).max() != T // E:
        load = np.bincount(second, minlength=E); hi, lo = int(load.argmax()), int(load.argmin())
        t = np.flatnonzero((second == hi) & (first != lo))[0]; second[t] = lo
    slot_token = np.empty(E * C, np.int64); pos = np.empty((2, T), np.int64); fill = np.zeros(E, np.int64)
    place = np.stack([np.random.permutation(C) for _ in range(E)])
    for r, deal in enumerate((first, second)):
        for t in np.random.permutation(T):
            e = deal[t]; j = e * C + place[e, fill[e]]; fill[e] += 1; slot_token[j] = t; pos[r, t] = j
    g = np.random.uniform(0.2, 0.8, T)
    return {
        "xT": (n((K, T)) * s).astype(np.float32),
        "w": (n((E, K, N)) / np.sqrt(K) / s[None]).astype(np.float32),
        "b": (0.3 * n((N, E))).astype(np.float32),
        "gate": np.stack([np.tile(g, (N, 1)), np.tile(1.0 - g, (N, 1))]).astype(np.float32),
        "offs": striped(slot_token),
        "pos1": striped(pos[0]),
        "pos2": striped(pos[1]),
    }


def reference(xT, w, b, gate, offs, pos1, pos2):
    idx = unstriped(offs)
    xq = mxq(f64(xT)[:, idx], 0, "e4m3")
    y = by_expert(mxq(f64(w), 1, "e4m3"), xq)
    y = relu2(y + np.repeat(f64(b), C, axis=1))
    return f64(gate[0]) * y[:, unstriped(pos1)] + f64(gate[1]) * y[:, unstriped(pos2)]

@@ -1,0 +1,185 @@
+from contextlib import ExitStack
+
+import concourse.mybir as mybir
+
+K, T, E, C, N = 512, 1536, 12, 256, 128
+SLOTS = E * C
+P = 128
+PACK = 4
+
+FLOPS = 2 * K * N * SLOTS
+
+F32 = mybir.dt.float32
+BF16 = mybir.dt.bfloat16
+U32 = mybir.dt.uint32
+U16 = mybir.dt.uint16
+U8 = mybir.dt.uint8
+I32 = mybir.dt.int32
+FP8X4 = mybir.dt.float8_e4m3fn_x4
+ACT = mybir.ActivationFunctionType
+MULT = mybir.AluOpType.mult
+ADD = mybir.AluOpType.add
+
+X_CHUNKS = (512, 512, 256, 256)
+SCALAR_SHARE = 5
+W_GROUP = 2
+OUT_CHUNKS = (512, 512, 320, 192)
+
+
+def spans(widths):
+    start = 0
+    result = []
+    for width in widths:
+        result.append((start, start + width))
+        start += width
+    return result
+
+
+def tile_routed_moe_kernel(tc, xT, w, b, gate, offs, pos1, pos2, out):
+    nc = tc.nc
+    with ExitStack() as ctx:
+        keep = ctx.enter_context(tc.tile_pool(name="keep", bufs=1))
+        psum = ctx.enter_context(tc.psum_pool(name="psum", bufs=1))
+
+        offs_sb = keep.tile([P, SLOTS // 16], U16, name="offs_sb")
+        pos1_sb = keep.tile([P, T // 16], U16, name="pos1_sb")
+        pos2_sb = keep.tile([P, T // 16], U16, name="pos2_sb")
+        b_sb = keep.tile([P, E], F32, name="b_sb")
+        gate_sb = [keep.tile([P, T], F32, name=f"gate{i}") for i in range(2)]
+
+        x_rows = xT.rearrange("(p j) t -> p j t", j=PACK)
+        x_raw = [keep.tile([P, PACK, n], F32, name=f"x_raw{i}") for i, n in enumerate(X_CHUNKS)]
+        w_rows = w.rearrange("e (p j) n -> p e (j n)", j=PACK)
+        w_raw = [keep.tile([P, W_GROUP, PACK * N], F32, name=f"w_raw{g}") for g in range(E // W_GROUP)]
+
+        for i, (lo, hi) in enumerate(spans(X_CHUNKS)):
+            nc.sync.dma_start(out=x_raw[i][:], in_=x_rows[:, :, lo:hi])
+            if i == 1:
+                nc.sync.dma_start(offs_sb[:], offs)
+        nc.sync.dma_start(out=b_sb[:], in_=b)
+        for g in range(E // W_GROUP):
+            nc.sync.dma_start(out=w_raw[g][:], in_=w_rows[:, g * W_GROUP:(g + 1) * W_GROUP, :])
+        nc.sync.dma_start(pos1_sb[:], pos1)
+        nc.sync.dma_start(pos2_sb[:], pos2)
+        for i in range(2):
+            nc.sync.dma_start(out=gate_sb[i][:], in_=gate[i])
+
+        x_codes = keep.tile([P, T], U32, name="x_codes", align_bytes=64)
+        x_scales = keep.tile([P, T], U8, name="x_scales", align_bytes=64)
+        nc.gpsimd.memset(x_scales[:], 0)
+
+        for i, (lo, hi) in enumerate(spans(X_CHUNKS)):
+            n = hi - lo
+            cut = n * (16 - SCALAR_SHARE) // 16
+            x_bf = keep.tile([P, n, PACK], BF16, name=f"x_bf{i}", align_bytes=64)
+            src = x_raw[i][:].rearrange("p j t -> p t j")
+            nc.vector.tensor_copy(out=x_bf[:, :cut, :], in_=src[:, :cut, :])
+            nc.scalar.copy(out=x_bf[:, cut:, :], in_=src[:, cut:, :])
+            nc.vector.quantize_mx(
+                out=x_codes[:, lo:hi].bitcast(FP8X4),
+                scales=x_scales[:, lo:hi],
+                in_=x_bf[:].rearrange("p t j -> p (t j)"),
+            )
+
+        shared = ctx.enter_context(tc.tile_pool(name="shared", bufs=1))
+        w_codes = []
+        w_scales = []
+        r_sb = keep.tile([P, SLOTS], F32, name="r_sb")
+        y_sb = keep.tile([P, SLOTS], F32, name="y_sb")
+
+        def gather(table, dtype, span, tag, name):
+            lo, hi = span
+            dst = shared.tile([P, hi - lo], dtype, name=name, tag=tag, align_bytes=64)
+            nc.vector.tensor_copy(dst[:], table[:].indirect(offs_sb[:, lo // 16:hi // 16]))
+            return dst
+
+        def gather_words(lo, hi, tag):
+            return gather(x_codes, U32, (lo, hi), tag, f"slot_words{lo}")
+
+        def gather_scales(lo, hi, tag):
+            return gather(x_scales, U8, (lo, hi), tag, f"slot_scales{lo}")
+
+        def quantize_weights(g):
+            w_bf = shared.tile([P, W_GROUP, N, PACK], BF16, name=f"w_bf{g}", tag=f"w_bf{g}", align_bytes=64)
+            for e in range(W_GROUP):
+                nc.scalar.copy(
+                    out=w_bf[:, e, :, :],
+                    in_=w_raw[g][:, e, :].rearrange("p (j n) -> p n j", j=PACK),
+                )
+            codes = keep.tile([P, W_GROUP * N], U32, name=f"w_codes{g}", align_bytes=64)
+            scales = keep.tile([P, W_GROUP * N], U8, name=f"w_scales{g}", align_bytes=64)
+            nc.vector.quantize_mx(
+                out=codes[:].bitcast(FP8X4),
+                scales=scales[:],
+                in_=w_bf[:].rearrange("p e n j -> p (e n j)"),
+            )
+            w_codes.append(codes)
+            w_scales.append(scales)
+
+        def experts(first, count, words, scales, base_words, base_scales):
+            bank = None
+            for e in range(first, first + count):
+                h = e % 2
+                if e % 2 == 0 or e == first:
+                    bank = psum.tile([P, C * (2 if count > 1 else 1)], F32, name=f"bank{e}")
+                    if count == 1 or (count == 3 and e == first + 2):
+                        h = 0
+                g, k = divmod(e, W_GROUP)
+                wcols = slice(k * N, (k + 1) * N)
+                cols = slice(e * C, (e + 1) * C)
+                ww = slice(e * C - base_words, (e + 1) * C - base_words)
+                ss = slice(e * C - base_scales, (e + 1) * C - base_scales)
+                nc.tensor.matmul_mx(
+                    out=bank[:, h * C:(h + 1) * C],
+                    lhsT=w_codes[g][:, wcols].bitcast(FP8X4),
+                    lhsT_scale=w_scales[g][:, wcols],
+                    rhs=words[:, ww].bitcast(FP8X4),
+                    rhs_scale=scales[:, ss],
+                    start=True,
+                    stop=True,
+                )
+                nc.scalar.activation(
+                    out=r_sb[:, cols], in_=bank[:, h * C:(h + 1) * C], func=ACT.Relu, bias=b_sb[:, e:e + 1]
+                )
+                nc.scalar.activation(out=y_sb[:, cols], in_=r_sb[:, cols], func=ACT.Square)
+
+        words = gather_words(0, 1024, "words0")
+        scales = gather_scales(0, 1024, "scales0")
+        quantize_weights(0)
+        quantize_weights(1)
+        experts(0, 4, words, scales, 0, 0)
+        words = gather_words(1024, 2048, "w_bf0")
+        scales = gather_scales(1024, 2048, "w_bf1")
+        quantize_weights(2)
+        quantize_weights(3)
+        experts(4, 4, words, scales, 1024, 1024)
+        words = gather_words(2048, 3072, "w_bf2")
+        quantize_weights(4)
+        quantize_weights(5)
+        scales = gather_scales(2048, 2816, "w_bf4")
+        experts(8, 3, words, scales, 2048, 2048)
+        scales = gather_scales(2816, 3072, "w_bf5")
+        experts(11, 1, words, scales, 2048, 2816)
+
+        out_sb = keep.tile([P, T], F32, name="out_sb")
+        prod = [keep.tile([P, T], F32, name=f"prod{i}") for i in range(2)]
+
+        def combine(i, span):
+            lo, hi = span
+            pos = (pos1_sb, pos2_sb)[i]
+            nc.vector.tensor_tensor(
+                prod[i][:, lo:hi], y_sb[:].indirect(pos[:, lo // 16:hi // 16]), gate_sb[i][:, lo:hi], MULT
+            )
+
+        def finish(span):
+            lo, hi = span
+            nc.vector.tensor_tensor(out_sb[:, lo:hi], prod[0][:, lo:hi], prod[1][:, lo:hi], ADD)
+            nc.sync.dma_start(out=out[:, lo:hi], in_=out_sb[:, lo:hi])
+
+        out_spans = spans(OUT_CHUNKS)
+        for i, span in enumerate(out_spans):
+            combine(0, span)
+            if i > 0:
+                finish(out_spans[i - 1])
+            combine(1, span)
+        finish(out_spans[-1])

@@ -1,6 +1,7 @@
 from contextlib import ExitStack
 
 import concourse.mybir as mybir
+from concourse.masks import make_identity
 
 K, T, E, C, N = 512, 1536, 12, 256, 128
 SLOTS = E * C
@@ -19,11 +20,12 @@ FP8X4 = mybir.dt.float8_e4m3fn_x4
 ACT = mybir.ActivationFunctionType
 MULT = mybir.AluOpType.mult
 ADD = mybir.AluOpType.add
+MAX = mybir.AluOpType.max
 
-X_CHUNKS = (512, 512, 256, 256)
-SCALAR_SHARE = 5
+X_CHUNKS = (512, 256, 256, 256, 256)
+SCALAR_SHARE = (6, 4, 4, 4, 4)
 W_GROUP = 2
-OUT_CHUNKS = (512, 512, 320, 192)
+OUT_CHUNKS = (512, 768, 256)
 
 
 def spans(widths):
@@ -64,13 +66,15 @@ def tile_routed_moe_kernel(tc, xT, w, b, gate, offs, pos1, pos2, out):
         for i in range(2):
             nc.sync.dma_start(out=gate_sb[i][:], in_=gate[i])
 
+        identity = keep.tile([P, P], F32, name="identity")
         x_codes = keep.tile([P, T], U32, name="x_codes", align_bytes=64)
         x_scales = keep.tile([P, T], U8, name="x_scales", align_bytes=64)
         nc.gpsimd.memset(x_scales[:], 0)
+        make_identity(nc, identity[:])
 
         for i, (lo, hi) in enumerate(spans(X_CHUNKS)):
             n = hi - lo
-            cut = n * (16 - SCALAR_SHARE) // 16
+            cut = n * (16 - SCALAR_SHARE[i]) // 16
             x_bf = keep.tile([P, n, PACK], BF16, name=f"x_bf{i}", align_bytes=64)
             src = x_raw[i][:].rearrange("p j t -> p t j")
             nc.vector.tensor_copy(out=x_bf[:, :cut, :], in_=src[:, :cut, :])
@@ -101,11 +105,11 @@ def tile_routed_moe_kernel(tc, xT, w, b, gate, offs, pos1, pos2, out):
 
         def quantize_weights(g):
             w_bf = shared.tile([P, W_GROUP, N, PACK], BF16, name=f"w_bf{g}", tag=f"w_bf{g}", align_bytes=64)
-            for e in range(W_GROUP):
-                nc.scalar.copy(
-                    out=w_bf[:, e, :, :],
-                    in_=w_raw[g][:, e, :].rearrange("p (j n) -> p n j", j=PACK),
-                )
+            src = w_raw[g][:].rearrange("p e (j n) -> p e n j", j=PACK)
+            if g % 2 == 0:
+                nc.scalar.copy(out=w_bf[:], in_=src)
+            else:
+                nc.gpsimd.tensor_scalar(w_bf[:], src, 1.0, 0.0, MULT, ADD)
             codes = keep.tile([P, W_GROUP * N], U32, name=f"w_codes{g}", align_bytes=64)
             scales = keep.tile([P, W_GROUP * N], U8, name=f"w_scales{g}", align_bytes=64)
             nc.vector.quantize_mx(
@@ -116,50 +120,74 @@ def tile_routed_moe_kernel(tc, xT, w, b, gate, offs, pos1, pos2, out):
             w_codes.append(codes)
             w_scales.append(scales)
 
-        def experts(first, count, words, scales, base_words, base_scales):
-            bank = None
-            for e in range(first, first + count):
-                h = e % 2
-                if e % 2 == 0 or e == first:
-                    bank = psum.tile([P, C * (2 if count > 1 else 1)], F32, name=f"bank{e}")
-                    if count == 1 or (count == 3 and e == first + 2):
-                        h = 0
-                g, k = divmod(e, W_GROUP)
-                wcols = slice(k * N, (k + 1) * N)
-                cols = slice(e * C, (e + 1) * C)
-                ww = slice(e * C - base_words, (e + 1) * C - base_words)
-                ss = slice(e * C - base_scales, (e + 1) * C - base_scales)
-                nc.tensor.matmul_mx(
-                    out=bank[:, h * C:(h + 1) * C],
-                    lhsT=w_codes[g][:, wcols].bitcast(FP8X4),
-                    lhsT_scale=w_scales[g][:, wcols],
-                    rhs=words[:, ww].bitcast(FP8X4),
-                    rhs_scale=scales[:, ss],
-                    start=True,
-                    stop=True,
-                )
-                nc.scalar.activation(
-                    out=r_sb[:, cols], in_=bank[:, h * C:(h + 1) * C], func=ACT.Relu, bias=b_sb[:, e:e + 1]
-                )
-                nc.scalar.activation(out=y_sb[:, cols], in_=r_sb[:, cols], func=ACT.Square)
+        banks = [psum.tile([P, 2 * C], F32, name=f"bank{g}") for g in range(5)]
+        banks.append(psum.tile([P, C], F32, name="bank5"))
+        banks.append(psum.tile([P, C], F32, name="bank6"))
+
+        def place(e):
+            return (banks[e // 2], e % 2) if e < 10 else (banks[e - 5], 0)
+
+        def matmul(e, words, scales, base):
+            bank, h = place(e)
+            g, k = divmod(e, W_GROUP)
+            wcols = slice(k * N, (k + 1) * N)
+            cols = slice(e * C - base, (e + 1) * C - base)
+            nc.tensor.matmul_mx(
+                out=bank[:, h * C:(h + 1) * C],
+                lhsT=w_codes[g][:, wcols].bitcast(FP8X4),
+                lhsT_scale=w_scales[g][:, wcols],
+                rhs=words[:, cols].bitcast(FP8X4),
+                rhs_scale=scales[:, cols],
+                start=True,
+                stop=True,
+            )
+
+        def relu(e):
+            bank, h = place(e)
+            nc.scalar.activation(
+                out=r_sb[:, e * C:(e + 1) * C], in_=bank[:, h * C:(h + 1) * C], func=ACT.Relu, bias=b_sb[:, e:e + 1]
+            )
+
+        def square(e, count):
+            done = slice(e * C, (e + count) * C)
+            nc.scalar.activation(out=y_sb[:, done], in_=r_sb[:, done], func=ACT.Square)
+
+        def relu2_vector(e):
+            bank, h = place(e)
+            done = slice(e * C, (e + 1) * C)
+            nc.vector.tensor_scalar(r_sb[:, done], bank[:, h * C:(h + 1) * C], b_sb[:, e:e + 1], 0.0, ADD, MAX)
+            nc.vector.tensor_tensor(y_sb[:, done], r_sb[:, done], r_sb[:, done], MULT)
+
+        def expert_pair(e, words, scales, base):
+            for i in range(2):
+                matmul(e + i, words, scales, base)
+                relu(e + i)
+            square(e, 2)
 
         words = gather_words(0, 1024, "words0")
         scales = gather_scales(0, 1024, "scales0")
         quantize_weights(0)
         quantize_weights(1)
-        experts(0, 4, words, scales, 0, 0)
+        expert_pair(0, words, scales, 0)
+        expert_pair(2, words, scales, 0)
         words = gather_words(1024, 2048, "w_bf0")
         scales = gather_scales(1024, 2048, "w_bf1")
         quantize_weights(2)
         quantize_weights(3)
-        experts(4, 4, words, scales, 1024, 1024)
-        words = gather_words(2048, 3072, "w_bf2")
+        expert_pair(4, words, scales, 1024)
+        expert_pair(6, words, scales, 1024)
+        words = gather_words(2048, 2560, "w_bf2")
         quantize_weights(4)
+        scales = gather_scales(2048, 2560, "w_bf3")
         quantize_weights(5)
-        scales = gather_scales(2048, 2816, "w_bf4")
-        experts(8, 3, words, scales, 2048, 2048)
-        scales = gather_scales(2816, 3072, "w_bf5")
-        experts(11, 1, words, scales, 2048, 2816)
+        expert_pair(8, words, scales, 2048)
+        words = gather_words(2560, 3072, "w_bf4")
+        scales = gather_scales(2560, 3072, "w_bf5")
+        matmul(11, words, scales, 2560)
+        matmul(10, words, scales, 2560)
+        relu(10)
+        square(10, 1)
+        relu2_vector(11)
 
         out_sb = keep.tile([P, T], F32, name="out_sb")
         prod = [keep.tile([P, T], F32, name=f"prod{i}") for i in range(2)]
@@ -171,6 +199,14 @@ def tile_routed_moe_kernel(tc, xT, w, b, gate, offs, pos1, pos2, out):
                 prod[i][:, lo:hi], y_sb[:].indirect(pos[:, lo // 16:hi // 16]), gate_sb[i][:, lo:hi], MULT
             )
 
+        def finish_on_tensor(span):
+            lo, hi = span
+            total = psum.tile([P, hi - lo], F32, name="total")
+            for i in range(2):
+                nc.tensor.matmul(total[:], identity[:], prod[i][:, lo:hi], start=(i == 0), stop=(i == 1))
+            nc.scalar.copy(out=out_sb[:, lo:hi], in_=total[:])
+            nc.sync.dma_start(out=out[:, lo:hi], in_=out_sb[:, lo:hi])
+
         def finish(span):
             lo, hi = span
             nc.vector.tensor_tensor(out_sb[:, lo:hi], prod[0][:, lo:hi], prod[1][:, lo:hi], ADD)
@@ -179,7 +215,9 @@ def tile_routed_moe_kernel(tc, xT, w, b, gate, offs, pos1, pos2, out):
         out_spans = spans(OUT_CHUNKS)
         for i, span in enumerate(out_spans):
             combine(0, span)
-            if i > 0:
-                finish(out_spans[i - 1])
+            if i == 2:
+                finish(out_spans[1])
             combine(1, span)
-        finish(out_spans[-1])
+            if i == 0:
+                finish_on_tensor(span)
+        finish(out_spans[2])

@@ -22,8 +22,8 @@ MULT = mybir.AluOpType.mult
 ADD = mybir.AluOpType.add
 MAX = mybir.AluOpType.max
 
-X_CHUNKS = (512, 256, 256, 256, 256)
-SCALAR_SHARE = (6, 4, 4, 4, 4)
+X_CHUNKS = (512, 512, 256, 256)
+SCALAR_SHARE = (6, 7, 6, 4)
 W_GROUP = 2
 OUT_CHUNKS = (512, 768, 256)
 
@@ -109,7 +109,8 @@ def tile_routed_moe_kernel(tc, xT, w, b, gate, offs, pos1, pos2, out):
             if g % 2 == 0:
                 nc.scalar.copy(out=w_bf[:], in_=src)
             else:
-                nc.gpsimd.tensor_scalar(w_bf[:], src, 1.0, 0.0, MULT, ADD)
+                for e in range(W_GROUP):
+                    nc.gpsimd.tensor_scalar(w_bf[:, e, :, :], src[:, e, :, :], 1.0, 0.0, MULT, ADD)
             codes = keep.tile([P, W_GROUP * N], U32, name=f"w_codes{g}", align_bytes=64)
             scales = keep.tile([P, W_GROUP * N], U8, name=f"w_scales{g}", align_bytes=64)
             nc.vector.quantize_mx(

from contextlib import ExitStack

import concourse.mybir as mybir
from concourse.masks import make_identity

K, T, E, C, N = 512, 1536, 12, 256, 128
SLOTS = E * C
P = 128
PACK = 4

FLOPS = 2 * K * N * SLOTS

F32 = mybir.dt.float32
BF16 = mybir.dt.bfloat16
U32 = mybir.dt.uint32
U16 = mybir.dt.uint16
U8 = mybir.dt.uint8
I32 = mybir.dt.int32
FP8X4 = mybir.dt.float8_e4m3fn_x4
ACT = mybir.ActivationFunctionType
MULT = mybir.AluOpType.mult
ADD = mybir.AluOpType.add
MAX = mybir.AluOpType.max

X_CHUNKS = (512, 512, 256, 256)
SCALAR_SHARE = (6, 7, 6, 4)
W_GROUP = 2
OUT_CHUNKS = (512, 768, 256)


def spans(widths):
    start = 0
    result = []
    for width in widths:
        result.append((start, start + width))
        start += width
    return result


def tile_routed_moe_kernel(tc, xT, w, b, gate, offs, pos1, pos2, out):
    nc = tc.nc
    with ExitStack() as ctx:
        keep = ctx.enter_context(tc.tile_pool(name="keep", bufs=1))
        psum = ctx.enter_context(tc.psum_pool(name="psum", bufs=1))

        offs_sb = keep.tile([P, SLOTS // 16], U16, name="offs_sb")
        pos1_sb = keep.tile([P, T // 16], U16, name="pos1_sb")
        pos2_sb = keep.tile([P, T // 16], U16, name="pos2_sb")
        b_sb = keep.tile([P, E], F32, name="b_sb")
        gate_sb = [keep.tile([P, T], F32, name=f"gate{i}") for i in range(2)]

        x_rows = xT.rearrange("(p j) t -> p j t", j=PACK)
        x_raw = [keep.tile([P, PACK, n], F32, name=f"x_raw{i}") for i, n in enumerate(X_CHUNKS)]
        w_rows = w.rearrange("e (p j) n -> p e (j n)", j=PACK)
        w_raw = [keep.tile([P, W_GROUP, PACK * N], F32, name=f"w_raw{g}") for g in range(E // W_GROUP)]

        for i, (lo, hi) in enumerate(spans(X_CHUNKS)):
            nc.sync.dma_start(out=x_raw[i][:], in_=x_rows[:, :, lo:hi])
            if i == 1:
                nc.sync.dma_start(offs_sb[:], offs)
        nc.sync.dma_start(out=b_sb[:], in_=b)
        for g in range(E // W_GROUP):
            nc.sync.dma_start(out=w_raw[g][:], in_=w_rows[:, g * W_GROUP:(g + 1) * W_GROUP, :])
        nc.sync.dma_start(pos1_sb[:], pos1)
        nc.sync.dma_start(pos2_sb[:], pos2)
        for i in range(2):
            nc.sync.dma_start(out=gate_sb[i][:], in_=gate[i])

        identity = keep.tile([P, P], F32, name="identity")
        x_codes = keep.tile([P, T], U32, name="x_codes", align_bytes=64)
        x_scales = keep.tile([P, T], U8, name="x_scales", align_bytes=64)
        nc.gpsimd.memset(x_scales[:], 0)
        make_identity(nc, identity[:])

        for i, (lo, hi) in enumerate(spans(X_CHUNKS)):
            n = hi - lo
            cut = n * (16 - SCALAR_SHARE[i]) // 16
            x_bf = keep.tile([P, n, PACK], BF16, name=f"x_bf{i}", align_bytes=64)
            src = x_raw[i][:].rearrange("p j t -> p t j")
            nc.vector.tensor_copy(out=x_bf[:, :cut, :], in_=src[:, :cut, :])
            nc.scalar.copy(out=x_bf[:, cut:, :], in_=src[:, cut:, :])
            nc.vector.quantize_mx(
                out=x_codes[:, lo:hi].bitcast(FP8X4),
                scales=x_scales[:, lo:hi],
                in_=x_bf[:].rearrange("p t j -> p (t j)"),
            )

        shared = ctx.enter_context(tc.tile_pool(name="shared", bufs=1))
        w_codes = []
        w_scales = []
        r_sb = keep.tile([P, SLOTS], F32, name="r_sb")
        y_sb = keep.tile([P, SLOTS], F32, name="y_sb")

        def gather(table, dtype, span, tag, name):
            lo, hi = span
            dst = shared.tile([P, hi - lo], dtype, name=name, tag=tag, align_bytes=64)
            nc.vector.tensor_copy(dst[:], table[:].indirect(offs_sb[:, lo // 16:hi // 16]))
            return dst

        def gather_words(lo, hi, tag):
            return gather(x_codes, U32, (lo, hi), tag, f"slot_words{lo}")

        def gather_scales(lo, hi, tag):
            return gather(x_scales, U8, (lo, hi), tag, f"slot_scales{lo}")

        def quantize_weights(g):
            w_bf = shared.tile([P, W_GROUP, N, PACK], BF16, name=f"w_bf{g}", tag=f"w_bf{g}", align_bytes=64)
            src = w_raw[g][:].rearrange("p e (j n) -> p e n j", j=PACK)
            if g % 2 == 0:
                nc.scalar.copy(out=w_bf[:], in_=src)
            else:
                for e in range(W_GROUP):
                    nc.gpsimd.tensor_scalar(w_bf[:, e, :, :], src[:, e, :, :], 1.0, 0.0, MULT, ADD)
            codes = keep.tile([P, W_GROUP * N], U32, name=f"w_codes{g}", align_bytes=64)
            scales = keep.tile([P, W_GROUP * N], U8, name=f"w_scales{g}", align_bytes=64)
            nc.vector.quantize_mx(
                out=codes[:].bitcast(FP8X4),
                scales=scales[:],
                in_=w_bf[:].rearrange("p e n j -> p (e n j)"),
            )
            w_codes.append(codes)
            w_scales.append(scales)

        banks = [psum.tile([P, 2 * C], F32, name=f"bank{g}") for g in range(5)]
        banks.append(psum.tile([P, C], F32, name="bank5"))
        banks.append(psum.tile([P, C], F32, name="bank6"))

        def place(e):
            return (banks[e // 2], e % 2) if e < 10 else (banks[e - 5], 0)

        def matmul(e, words, scales, base):
            bank, h = place(e)
            g, k = divmod(e, W_GROUP)
            wcols = slice(k * N, (k + 1) * N)
            cols = slice(e * C - base, (e + 1) * C - base)
            nc.tensor.matmul_mx(
                out=bank[:, h * C:(h + 1) * C],
                lhsT=w_codes[g][:, wcols].bitcast(FP8X4),
                lhsT_scale=w_scales[g][:, wcols],
                rhs=words[:, cols].bitcast(FP8X4),
                rhs_scale=scales[:, cols],
                start=True,
                stop=True,
            )

        def relu(e):
            bank, h = place(e)
            nc.scalar.activation(
                out=r_sb[:, e * C:(e + 1) * C], in_=bank[:, h * C:(h + 1) * C], func=ACT.Relu, bias=b_sb[:, e:e + 1]
            )

        def square(e, count):
            done = slice(e * C, (e + count) * C)
            nc.scalar.activation(out=y_sb[:, done], in_=r_sb[:, done], func=ACT.Square)

        def relu2_vector(e):
            bank, h = place(e)
            done = slice(e * C, (e + 1) * C)
            nc.vector.tensor_scalar(r_sb[:, done], bank[:, h * C:(h + 1) * C], b_sb[:, e:e + 1], 0.0, ADD, MAX)
            nc.vector.tensor_tensor(y_sb[:, done], r_sb[:, done], r_sb[:, done], MULT)

        def expert_pair(e, words, scales, base):
            for i in range(2):
                matmul(e + i, words, scales, base)
                relu(e + i)
            square(e, 2)

        words = gather_words(0, 1024, "words0")
        scales = gather_scales(0, 1024, "scales0")
        quantize_weights(0)
        quantize_weights(1)
        expert_pair(0, words, scales, 0)
        expert_pair(2, words, scales, 0)
        words = gather_words(1024, 2048, "w_bf0")
        scales = gather_scales(1024, 2048, "w_bf1")
        quantize_weights(2)
        quantize_weights(3)
        expert_pair(4, words, scales, 1024)
        expert_pair(6, words, scales, 1024)
        words = gather_words(2048, 2560, "w_bf2")
        quantize_weights(4)
        scales = gather_scales(2048, 2560, "w_bf3")
        quantize_weights(5)
        expert_pair(8, words, scales, 2048)
        words = gather_words(2560, 3072, "w_bf4")
        scales = gather_scales(2560, 3072, "w_bf5")
        matmul(11, words, scales, 2560)
        matmul(10, words, scales, 2560)
        relu(10)
        square(10, 1)
        relu2_vector(11)

        out_sb = keep.tile([P, T], F32, name="out_sb")
        prod = [keep.tile([P, T], F32, name=f"prod{i}") for i in range(2)]

        def combine(i, span):
            lo, hi = span
            pos = (pos1_sb, pos2_sb)[i]
            nc.vector.tensor_tensor(
                prod[i][:, lo:hi], y_sb[:].indirect(pos[:, lo // 16:hi // 16]), gate_sb[i][:, lo:hi], MULT
            )

        def finish_on_tensor(span):
            lo, hi = span
            total = psum.tile([P, hi - lo], F32, name="total")
            for i in range(2):
                nc.tensor.matmul(total[:], identity[:], prod[i][:, lo:hi], start=(i == 0), stop=(i == 1))
            nc.scalar.copy(out=out_sb[:, lo:hi], in_=total[:])
            nc.sync.dma_start(out=out[:, lo:hi], in_=out_sb[:, lo:hi])

        def finish(span):
            lo, hi = span
            nc.vector.tensor_tensor(out_sb[:, lo:hi], prod[0][:, lo:hi], prod[1][:, lo:hi], ADD)
            nc.sync.dma_start(out=out[:, lo:hi], in_=out_sb[:, lo:hi])

        out_spans = spans(OUT_CHUNKS)
        for i, span in enumerate(out_spans):
            combine(0, span)
            if i == 2:
                finish(out_spans[1])
            combine(1, span)
            if i == 0:
                finish_on_tensor(span)
        finish(out_spans[2])
